import numpy as np
import ml_dtypes


def mxq(x, axis, fmt="e4m3"):
    dtype, down = {"e4m3": (ml_dtypes.float8_e4m3fn, 7), "e5m2": (ml_dtypes.float8_e5m2, 14)}[fmt]
    v = np.moveaxis(np.asarray(x, np.float32).astype(ml_dtypes.bfloat16).astype(np.float64), axis, -1)
    blocks = v.reshape(v.shape[:-1] + (-1, 32))
    amax = np.abs(blocks).max(-1, keepdims=True)
    byte = np.maximum(np.where(amax > 0, np.frexp(amax)[1] - 1 + 127, 0) - down, 1)
    scale = np.exp2(byte - 127.0)
    codes = (blocks / scale).astype(np.float32).astype(dtype).astype(np.float64)
    return np.moveaxis((codes * scale).reshape(v.shape), -1, axis)


WIDE = False


def mx_kscale(k):
    if not WIDE:
        return np.ones(k)
    levels = np.array([10, -10, 5, -5, 0])
    if k % 512:
        return np.exp2(np.random.permutation(np.resize(levels, k // 32))).repeat(32)
    a = np.empty((k // 512, 16))
    for p in range(k // 512):
        a[p, :8] = np.random.permutation(np.resize(levels, 8))
        for g in range(8):
            far = levels[np.abs(levels - a[p, g]) >= 10]
            a[p, g + 8] = far[np.random.randint(len(far))]
    return np.exp2(a.ravel()).repeat(32)


def f64(x):
    return np.asarray(x).astype(np.float64)


def striped(idx):
    return np.tile(idx.reshape(-1, 16).T, (8, 1)).astype(np.uint16)


def unstriped(offs):
    return offs[:16].T.reshape(-1).astype(np.int64)


E2M1 = np.array([0.0, 0.5, 1.0, 1.5, 2.0, 3.0, 4.0, 6.0, -0.0, -0.5, -1.0, -1.5, -2.0, -3.0, -4.0, -6.0])


def pack_weight(w, fmt):
    k, n = w.shape
    w = f64(np.asarray(w, np.float32).astype(ml_dtypes.bfloat16)).reshape(k // 32, 32, n)
    amax = np.abs(w).max(1)
    if fmt == "e4m3":
        byte = np.frexp(amax)[1] - 1 + 127 - 7
    else:
        mant, ex = np.frexp(amax / 6.0)
        byte = np.where(mant > 0.5, ex, ex - 1) + 127
    byte = np.clip(np.where(amax > 0, byte, 1), 1, 254)
    scaled = (w * np.exp2(127.0 - byte)[:, None, :]).reshape(k, n).astype(np.float32)
    by_word = np.ascontiguousarray(scaled.reshape(k // 512, 128, 4, n).transpose(0, 1, 3, 2))
    if fmt == "e4m3":
        words = by_word.astype(ml_dtypes.float8_e4m3fn).view(np.uint8)
    else:
        c = by_word.astype(ml_dtypes.float4_e2m1fn).view(np.uint8) & 0xF
        words = (c[..., 0::2] | (c[..., 1::2] << 4)).reshape(k // 512, 128, 2 * n)
    return np.ascontiguousarray(words), np.ascontiguousarray(byte.astype(np.uint8).reshape(k // 512, 16, n))


def unpack_weight(words, scales, fmt):
    g, _, n = scales.shape
    words = np.ascontiguousarray(words).reshape(g, 128, n, -1)
    if fmt == "e4m3":
        vals = words.view(ml_dtypes.float8_e4m3fn).astype(np.float64)
    else:
        nib = np.empty((g, 128, n, 4), np.uint8)
        nib[..., 0::2] = words & 0xF
        nib[..., 1::2] = words >> 4
        vals = E2M1[nib]
    vals = vals * np.repeat(np.exp2(scales.astype(np.float64) - 127.0), 8, axis=1)[..., None]
    return vals.transpose(0, 1, 3, 2).reshape(g * 512, n)


def gelu(v):
    return 0.5 * v * (1.0 + np.tanh(np.sqrt(2.0 / np.pi) * (v + 0.044715 * v**3)))


K, T, S, P, H, N = 1024, 4096, 1024, 512, 512, 768

def setup_inputs():
    n = np.random.standard_normal
    s = mx_kscale(K)[:, None]
    u = mx_kscale(H)[:, None]
    tab_words, tab_scales = pack_weight(n((K, T)) * s, "e4m3")
    w2_words, w2_scales = pack_weight(0.5 * n((K, H)) / np.sqrt(K) / s, "e2m1")
    w4_words, w4_scales = pack_weight(n((H, N)) / np.sqrt(H) / u, "e2m1")
    return {
        "tab_words": tab_words, "tab_scales": tab_scales,
        "offs": striped(np.random.permutation(T)[:S]),
        "pos1": striped(np.random.permutation(S)[:P]),
        "pos2": striped(np.random.permutation(S)[:P]),
        "w1": (0.52 * n((K, H)) / np.sqrt(K) / s).astype(np.float32),
        "w2_words": w2_words, "w2_scales": w2_scales,
        "gain": (1.5 * np.exp(0.4 * n(H)) * u[:, 0]).astype(np.float32),
        "base": (0.6 * n(H) * u[:, 0]).astype(np.float32),
        "wash": (0.7 * n((H, P)) * u).astype(np.float32),
        "w3": (1.2 * n((H, N)) / np.sqrt(H) / u).astype(np.float32),
        "w4_words": w4_words, "w4_scales": w4_scales,
    }

def reference(tab_words, tab_scales, offs, pos1, pos2, w1, w2_words, w2_scales,
              gain, base, wash, w3, w4_words, w4_scales):
    v = unpack_weight(tab_words, tab_scales, "e4m3")[:, unstriped(offs)]
    w2 = unpack_weight(w2_words, w2_scales, "e2m1")
    w4 = unpack_weight(w4_words, w4_scales, "e2m1")
    e1 = mxq(f64(w1), 0, "e4m3").T @ v
    e2 = w2.T @ v
    h = (e1 * np.cos(e1) + e2) * f64(gain)[:, None]
    xa = np.maximum(h[:, unstriped(pos1)], f64(base)[:, None])
    xb = h[:, unstriped(pos2)] + f64(wash)
    ya = mxq(f64(w3), 0, "e4m3").T @ mxq(xa, 0, "e4m3")
    yb = w4.T @ mxq(xb, 0, "e4m3")
    return np.minimum(ya, yb)

@@ -1,0 +1,276 @@
+import math
+from contextlib import ExitStack
+
+import concourse.mybir as mybir
+
+K, T, S, P, H, N = 1024, 4096, 1024, 512, 512, 768
+FLOPS = 2 * 2 * K * H * S + 2 * 2 * H * N * P
+
+F32 = mybir.dt.float32
+BF16 = mybir.dt.bfloat16
+I32 = mybir.dt.int32
+U32 = mybir.dt.uint32
+U16 = mybir.dt.uint16
+U8 = mybir.dt.uint8
+E4M3 = mybir.dt.float8_e4m3fn_x4
+E2M1 = mybir.dt.float4_e2m1fn_x4
+ALU = mybir.AluOpType
+ACT = mybir.ActivationFunctionType
+
+PARTS = 128
+PACK = 4
+PASSES = K // 512
+BANK = 512
+HALF = P // 2
+LINEAR_AHEAD = 5
+
+
+def tile_list_hair_segment_readings_kernel(
+    tc, tab_words, tab_scales, offs, pos1, pos2, w1, w2_words, w2_scales,
+    gain, base, wash, w3, w4_words, w4_scales, out,
+):
+    nc = tc.nc
+    with ExitStack() as ctx:
+        keep = ctx.enter_context(tc.tile_pool(name="keep", bufs=1))
+        work = ctx.enter_context(tc.tile_pool(name="work", bufs=4))
+        psum = ctx.enter_context(tc.psum_pool(name="psum", bufs=8))
+
+        def held(shape, dtype, name, tag=None):
+            return keep.tile(shape, dtype, name=name, tag=tag or name, align_bytes=64)
+
+        offs_t = held([PARTS, S // 16], U16, "offs_t")
+        pos1_t = held([PARTS, P // 16], U16, "pos1_t")
+        pos2_t = held([PARTS, P // 16], U16, "pos2_t")
+        table0 = held([PARTS, T], U32, "table0", "slot_d")
+        table_scales = held([PARTS, T], U8, "table_scales", "slot_c")
+        w2_raw = [held([PARTS, 2 * H], U8, f"w2_raw{a}", ("slot_a", "slot_e")[a]) for a in range(PASSES)]
+        w4_plane = held([PARTS, N], U8, "w4_plane")
+        gain_t = held([PARTS, PACK], F32, "gain_t")
+        base_t = held([PARTS, PACK], F32, "base_t")
+        moved_scales = held([PARTS, S], U8, "moved_scales")
+
+        nc.vector.memset(table_scales[:].bitcast(I32), 0)
+        nc.vector.memset(moved_scales[:].bitcast(I32), 0)
+        nc.gpsimd.memset(w4_plane[:].bitcast(I32), 0)
+        nc.sync.dma_start(offs_t[:], offs)
+        for a in range(PASSES):
+            nc.sync.dma_start(w2_raw[a][:].bitcast(I32), w2_words[a].bitcast(I32))
+        nc.sync.dma_start(table0[:].bitcast(I32), tab_words[0].rearrange("p t i -> p (t i)").bitcast(I32))
+        for q in range(4):
+            nc.sync.dma_start(
+                table_scales[32 * q : 32 * q + 8, :].bitcast(I32),
+                tab_scales[:, 4 * q : 4 * q + 4, :].bitcast(I32),
+            )
+        nc.sync.dma_start(pos1_t[:], pos1)
+        nc.sync.dma_start(pos2_t[:], pos2)
+
+        w2_codes = held([PARTS, PASSES, 2 * H], U8, "w2_codes")
+        w2_plane = held([PARTS, PASSES, PACK, 128], U8, "w2_plane")
+        for a in range(PASSES):
+            nc.vector.tensor_copy(
+                w2_codes[:, a, :].rearrange("p (t m b) -> p m t b", t=PACK, b=2),
+                w2_raw[a][:].rearrange("p (m t b) -> p m t b", t=PACK, b=2),
+            )
+        table1 = held([PARTS, T], U32, "table1", "slot_a")
+        nc.sync.dma_start(table1[:].bitcast(I32), tab_words[1].rearrange("p t i -> p (t i)").bitcast(I32))
+        table = [table0, table1]
+        w2_scales_raw = held([PARTS, PASSES, H], U8, "w2_scales_raw", "slot_e")
+        nc.vector.memset(w2_scales_raw[:].bitcast(I32), 0)
+        for q in range(4):
+            nc.scalar.dma_start(
+                w2_scales_raw[32 * q : 32 * q + 4, :, :].bitcast(I32),
+                w2_scales[:, 4 * q : 4 * q + 4, :].rearrange("a r c -> r a c").bitcast(I32),
+            )
+        nc.vector.tensor_copy(
+            w2_plane[:].rearrange("p a t m -> p a m t"),
+            w2_scales_raw[:].rearrange("p a (m t) -> p a m t", t=PACK),
+        )
+        nc.gpsimd.dma_start(gain_t[:], gain.rearrange("(p t) -> p t", t=PACK))
+        nc.gpsimd.dma_start(base_t[:], base.rearrange("(p t) -> p t", t=PACK))
+        for q in range(4):
+            nc.gpsimd.dma_start(
+                w4_plane[32 * q : 32 * q + 4, :].bitcast(I32),
+                w4_scales[0, 4 * q : 4 * q + 4, :].bitcast(I32),
+            )
+        w1_rows = w1.rearrange("(a p j) c -> a p j c", a=PASSES, j=PACK)
+
+        picked = [[held([PARTS, BANK], U32, f"picked{a}{hf}") for hf in range(2)] for a in range(PASSES)]
+
+        def pick_words(a):
+            for hf in range(2):
+                nc.vector.tensor_copy(
+                    picked[a][hf][:], table[a][:].indirect(offs_t[:, hf * 32 : (hf + 1) * 32])
+                )
+
+        pick_words(0)
+        w1_raw0 = held([PARTS, PACK, H], F32, "w1_raw0", "slot_d")
+        nc.sync.dma_start(w1_raw0[:], w1_rows[0])
+        picked_scales = held([PARTS, S], U8, "picked_scales")
+        nc.vector.tensor_copy(picked_scales[:], table_scales[:].indirect(offs_t[:]))
+        nc.scalar.dma_start(moved_scales[0:112, :].bitcast(I32), picked_scales[4:116, :].bitcast(I32))
+        picked_plane = [picked_scales, moved_scales]
+        w1_raw1 = held([PARTS, 2, PACK, H // 2], F32, "w1_raw1", "slot_c")
+        for c in range(2):
+            nc.sync.dma_start(w1_raw1[:, c], w1_rows[1][:, :, c * (H // 2) : (c + 1) * (H // 2)])
+        pick_words(1)
+        wash_t = held([PARTS, PACK, P], F32, "wash_t", "slot_a")
+        nc.sync.dma_start(wash_t[:], wash.rearrange("(p t) j -> p t j", t=PACK))
+
+        linear = [held([PARTS, S], F32, f"linear{t}") for t in range(PACK)]
+
+        def linear_part(unit):
+            t, hf = divmod(unit, 2)
+            cols = slice(hf * BANK, (hf + 1) * BANK)
+            e2 = psum.tile([PARTS, BANK], F32, name="e2", tag="bank")
+            for a in range(PASSES):
+                nc.tensor.matmul_mx(
+                    e2[:], w2_codes[:, a, 256 * t : 256 * (t + 1)].bitcast(E2M1), w2_plane[:, a, t, :],
+                    picked[a][hf][:].bitcast(E4M3), picked_plane[a][:, cols],
+                    start=(a == 0), stop=(a == PASSES - 1),
+                )
+            nc.scalar.activation(linear[t][:, cols], e2[:], ACT.Copy, scale=gain_t[:, t : t + 1])
+
+        for unit in range(LINEAR_AHEAD):
+            linear_part(unit)
+
+        w1_bf = [held([PARTS, PACK, 128, PACK], BF16, f"w1_bf{a}", ("slot_b", "slot_f")[a]) for a in range(PASSES)]
+        w1_codes = [held([PARTS, H], U32, f"w1_codes{a}") for a in range(PASSES)]
+        w1_plane = [held([PARTS, H], U8, f"w1_plane{a}") for a in range(PASSES)]
+        nc.vector.tensor_copy(
+            w1_bf[0][:].rearrange("p t m j -> p m t j"),
+            w1_raw0[:].rearrange("p j (m t) -> p m t j", t=PACK),
+        )
+        nc.vector.quantize_mx(
+            w1_codes[0][:].bitcast(E4M3), w1_plane[0][:], w1_bf[0][:].rearrange("p t m j -> p (t m j)")
+        )
+        for c in range(2):
+            nc.vector.tensor_copy(
+                w1_bf[1][:, :, c * 64 : (c + 1) * 64, :].rearrange("p t m j -> p m t j"),
+                w1_raw1[:, c].rearrange("p j (m t) -> p m t j", t=PACK),
+            )
+        w1_flat = w1_bf[1][:].rearrange("p t m j -> p (t m j)")
+        for lo, hi in ((0, 128), (128, H)):
+            nc.vector.quantize_mx(
+                w1_codes[1][:, lo:hi].bitcast(E4M3), w1_plane[1][:, lo:hi], w1_flat[:, PACK * lo : PACK * hi]
+            )
+
+        w3_rows = w3.rearrange("(p t) n -> p t n", t=PACK)
+        w3_raw = [held([PARTS, PACK, N // 2], F32, f"w3_raw{c}", ("slot_d", "slot_c")[c]) for c in range(2)]
+        for c in range(2):
+            nc.sync.dma_start(w3_raw[c][:], w3_rows[:, :, c * (N // 2) : (c + 1) * (N // 2)])
+        w4_codes = held([PARTS, 2 * N], U8, "w4_codes", "slot_b")
+        nc.sync.dma_start(w4_codes[:].bitcast(I32), w4_words[0].bitcast(I32))
+
+        h = [held([PARTS, S], F32, f"h{t}") for t in range(PACK)]
+        xa = held([PARTS, P, PACK], BF16, "xa")
+        xb = held([PARTS, P, PACK], BF16, "xb")
+        xa_low = held([PARTS, 2, P], BF16, "xa_low")
+        xb_f32 = [held([PARTS, 2, P], F32, f"xb_f32{u}") for u in range(2)]
+        near = [held([PARTS, P], F32, f"near{t}") for t in range(PACK)]
+        w3_bf = held([PARTS, N, PACK], BF16, "w3_bf")
+        w3_codes = held([PARTS, N], U32, "w3_codes")
+        w3_plane = held([PARTS, N], U8, "w3_plane")
+
+        def features(t, hf):
+            cols = slice(hf * BANK, (hf + 1) * BANK)
+            rows = slice(t * 128, (t + 1) * 128)
+            e1 = psum.tile([PARTS, BANK], F32, name="e1", tag="bank")
+            for a in range(PASSES):
+                nc.tensor.matmul_mx(
+                    e1[:], w1_codes[a][:, rows].bitcast(E4M3), w1_plane[a][:, rows],
+                    picked[a][hf][:].bitcast(E4M3), picked_plane[a][:, cols],
+                    start=(a == 0), stop=(a == PASSES - 1),
+                )
+            turns = work.tile([PARTS, BANK], F32, name="turns")
+            whole = work.tile([PARTS, BANK], I32, name="whole")
+            rest = work.tile([PARTS, BANK], F32, name="rest")
+            if hf == 0 and t > 0:
+                cosine = near[t - 1]
+                wave = xb_f32[(t - 1) // 2][:, (t - 1) % 2, :]
+            else:
+                cosine = work.tile([PARTS, BANK], F32, name="cosine")
+                wave_tile = work.tile([PARTS, BANK], F32, name="wave_tile")
+                wave = wave_tile[:]
+            nc.scalar.activation(turns[:], e1[:], ACT.Copy, bias=0.25, scale=1.0 / (2.0 * math.pi))
+            nc.gpsimd.tensor_scalar(whole[:], turns[:], 1.0, 0.0, ALU.mult, ALU.add)
+            nc.vector.scalar_tensor_tensor(rest[:], whole[:], -2.0 * math.pi, e1[:], ALU.mult, ALU.add)
+            nc.scalar.activation(cosine[:], rest[:], ACT.Sin, bias=math.pi / 2.0, scale=1.0)
+            nc.vector.scalar_tensor_tensor(wave, cosine[:], gain_t[:, t : t + 1], e1[:], ALU.mult, ALU.mult)
+            nc.gpsimd.tensor_tensor(h[t][:, cols], wave, linear[t][:, cols], ALU.add)
+
+        def pick(t, lo, hi):
+            entries = slice(lo // 16, hi // 16)
+            nc.vector.tensor_copy(near[t][:, lo:hi], h[t][:].indirect(pos1_t[:, entries]))
+            target = xa_low[:, t, lo:hi] if t < 2 else xa[:, lo:hi, t]
+            nc.vector.tensor_tensor(
+                xb_f32[t // 2][:, t % 2, lo:hi], h[t][:].indirect(pos2_t[:, entries]), wash_t[:, t, lo:hi], ALU.add
+            )
+            nc.vector.tensor_scalar_max(target, near[t][:, lo:hi], base_t[:, t : t + 1])
+
+        def weave_xb(u, lo, hi):
+            nc.scalar.copy(xb[:, lo:hi, 2 * u : 2 * u + 2], xb_f32[u][:, :, lo:hi].rearrange("p t j -> p j t"))
+
+        def weave_w3(c):
+            nc.scalar.copy(
+                w3_bf[:, c * (N // 2) : (c + 1) * (N // 2), :].rearrange("p (g i) t -> p g t i", i=4),
+                w3_raw[c][:].rearrange("p t (g i) -> p g t i", i=4),
+            )
+
+        def quantise_w3(c):
+            cols = slice(c * (N // 2), (c + 1) * (N // 2))
+            nc.vector.quantize_mx(
+                w3_codes[:, cols].bitcast(E4M3), w3_plane[:, cols], w3_bf[:, cols, :].rearrange("p n t -> p (n t)")
+            )
+
+        for t in range(PACK):
+            for hf in range(2):
+                features(t, hf)
+                if 2 * t + hf + LINEAR_AHEAD < 2 * PACK:
+                    linear_part(2 * t + hf + LINEAR_AHEAD)
+            if t >= 1:
+                pick(t - 1, 0, P)
+            if t == 2:
+                nc.scalar.copy(xa[:, :, 0:2], xa_low[:].rearrange("p t j -> p j t"))
+                weave_xb(0, 0, P)
+            if t in (1, 2):
+                weave_w3(t - 1)
+            if t >= 2:
+                quantise_w3(t - 2)
+
+        xa_codes = held([PARTS, P], U32, "xa_codes")
+        xb_codes = held([PARTS, P], U32, "xb_codes")
+        xa_plane = held([PARTS, P], U8, "xa_plane")
+        xb_plane = held([PARTS, P], U8, "xb_plane")
+        for hf in range(2):
+            pick(PACK - 1, hf * HALF, (hf + 1) * HALF)
+            weave_xb(1, hf * HALF, (hf + 1) * HALF)
+        for hf in range(2):
+            cols = slice(hf * HALF, (hf + 1) * HALF)
+            for codes, plane, x in ((xa_codes, xa_plane, xa), (xb_codes, xb_plane, xb)):
+                nc.vector.quantize_mx(
+                    codes[:, cols].bitcast(E4M3), plane[:, cols], x[:, cols, :].rearrange("p j t -> p (j t)")
+                )
+        for hf in range(2):
+            cols = slice(hf * HALF, (hf + 1) * HALF)
+            for pair in range(N // 256):
+                ya = psum.tile([PARTS, 2, HALF], F32, name="ya", tag="bank")
+                yb = psum.tile([PARTS, 2, HALF], F32, name="yb", tag="bank")
+                for i in range(2):
+                    n0 = (2 * pair + i) * 128
+                    nc.tensor.matmul_mx(
+                        ya[:, i, :], w3_codes[:, n0 : n0 + 128].bitcast(E4M3), w3_plane[:, n0 : n0 + 128],
+                        xa_codes[:, cols].bitcast(E4M3), xa_plane[:, cols], start=True, stop=True,
+                    )
+                for i in range(2):
+                    n0 = (2 * pair + i) * 128
+                    nc.tensor.matmul_mx(
+                        yb[:, i, :], w4_codes[:, 2 * n0 : 2 * n0 + 256].bitcast(E2M1), w4_plane[:, n0 : n0 + 128],
+                        xb_codes[:, cols].bitcast(E4M3), xb_plane[:, cols], start=True, stop=True,
+                    )
+                ya_s = work.tile([PARTS, 2, HALF], F32, name="ya_s")
+                score = work.tile([PARTS, 2, HALF], F32, name="score")
+                nc.scalar.copy(ya_s[:], ya[:])
+                nc.vector.tensor_tensor(score[:], ya_s[:], yb[:], ALU.min)
+                nc.sync.dma_start(
+                    out[pair * 256 : (pair + 1) * 256, cols].rearrange("(i p) j -> p i j", i=2), score[:]
+                )

@@ -22,7 +22,7 @@ PACK = 4
 PASSES = K // 512
 BANK = 512
 HALF = P // 2
-LINEAR_AHEAD = 5
+ROUNDER = 1.5 * 2.0**23
 
 
 def tile_list_hair_segment_readings_kernel(
@@ -33,7 +33,8 @@ def tile_list_hair_segment_readings_kernel(
     with ExitStack() as ctx:
         keep = ctx.enter_context(tc.tile_pool(name="keep", bufs=1))
         work = ctx.enter_context(tc.tile_pool(name="work", bufs=4))
-        psum = ctx.enter_context(tc.psum_pool(name="psum", bufs=8))
+        over = ctx.enter_context(tc.tile_pool(name="over", bufs=1))
+        psum = ctx.enter_context(tc.psum_pool(name="psum", bufs=1))
 
         def held(shape, dtype, name, tag=None):
             return keep.tile(shape, dtype, name=name, tag=tag or name, align_bytes=64)
@@ -41,8 +42,8 @@ def tile_list_hair_segment_readings_kernel(
         offs_t = held([PARTS, S // 16], U16, "offs_t")
         pos1_t = held([PARTS, P // 16], U16, "pos1_t")
         pos2_t = held([PARTS, P // 16], U16, "pos2_t")
-        table0 = held([PARTS, T], U32, "table0", "slot_d")
-        table_scales = held([PARTS, T], U8, "table_scales", "slot_c")
+        table0 = held([PARTS, T], U32, "table0")
+        table_scales = over.tile([PARTS, T], U8, name="table_scales", offset=0, align_bytes=64)
         w2_raw = [held([PARTS, 2 * H], U8, f"w2_raw{a}", ("slot_a", "slot_e")[a]) for a in range(PASSES)]
         w4_plane = held([PARTS, N], U8, "w4_plane")
         gain_t = held([PARTS, PACK], F32, "gain_t")
@@ -65,11 +66,10 @@ def tile_list_hair_segment_readings_kernel(
         nc.sync.dma_start(pos2_t[:], pos2)
 
         w2_codes = held([PARTS, PASSES, 2 * H], U8, "w2_codes")
-        w2_plane = held([PARTS, PASSES, PACK, 128], U8, "w2_plane")
         for a in range(PASSES):
             nc.vector.tensor_copy(
-                w2_codes[:, a, :].rearrange("p (t m b) -> p m t b", t=PACK, b=2),
-                w2_raw[a][:].rearrange("p (m t b) -> p m t b", t=PACK, b=2),
+                w2_codes[:, a, :].rearrange("p (t m b) -> p t m b", t=PACK, b=2),
+                w2_raw[a][:].rearrange("p (m t b) -> p t m b", t=PACK, b=2),
             )
         table1 = held([PARTS, T], U32, "table1", "slot_a")
         nc.sync.dma_start(table1[:].bitcast(I32), tab_words[1].rearrange("p t i -> p (t i)").bitcast(I32))
@@ -77,14 +77,10 @@ def tile_list_hair_segment_readings_kernel(
         w2_scales_raw = held([PARTS, PASSES, H], U8, "w2_scales_raw", "slot_e")
         nc.vector.memset(w2_scales_raw[:].bitcast(I32), 0)
         for q in range(4):
-            nc.scalar.dma_start(
+            nc.sync.dma_start(
                 w2_scales_raw[32 * q : 32 * q + 4, :, :].bitcast(I32),
                 w2_scales[:, 4 * q : 4 * q + 4, :].rearrange("a r c -> r a c").bitcast(I32),
             )
-        nc.vector.tensor_copy(
-            w2_plane[:].rearrange("p a t m -> p a m t"),
-            w2_scales_raw[:].rearrange("p a (m t) -> p a m t", t=PACK),
-        )
         nc.gpsimd.dma_start(gain_t[:], gain.rearrange("(p t) -> p t", t=PACK))
         nc.gpsimd.dma_start(base_t[:], base.rearrange("(p t) -> p t", t=PACK))
         for q in range(4):
@@ -94,7 +90,10 @@ def tile_list_hair_segment_readings_kernel(
             )
         w1_rows = w1.rearrange("(a p j) c -> a p j c", a=PASSES, j=PACK)
 
-        picked = [[held([PARTS, BANK], U32, f"picked{a}{hf}") for hf in range(2)] for a in range(PASSES)]
+        picked = [
+            [held([PARTS, BANK], U32, "picked00"), over.tile([PARTS, BANK], U32, name="picked01", offset=0, align_bytes=64)],
+            [held([PARTS, BANK], U32, "picked10"), held([PARTS, BANK], U32, "picked11")],
+        ]
 
         def pick_words(a):
             for hf in range(2):
@@ -102,52 +101,38 @@ def tile_list_hair_segment_readings_kernel(
                     picked[a][hf][:], table[a][:].indirect(offs_t[:, hf * 32 : (hf + 1) * 32])
                 )
 
-        pick_words(0)
-        w1_raw0 = held([PARTS, PACK, H], F32, "w1_raw0", "slot_d")
-        nc.sync.dma_start(w1_raw0[:], w1_rows[0])
         picked_scales = held([PARTS, S], U8, "picked_scales")
         nc.vector.tensor_copy(picked_scales[:], table_scales[:].indirect(offs_t[:]))
         nc.scalar.dma_start(moved_scales[0:112, :].bitcast(I32), picked_scales[4:116, :].bitcast(I32))
-        picked_plane = [picked_scales, moved_scales]
-        w1_raw1 = held([PARTS, 2, PACK, H // 2], F32, "w1_raw1", "slot_c")
-        for c in range(2):
-            nc.sync.dma_start(w1_raw1[:, c], w1_rows[1][:, :, c * (H // 2) : (c + 1) * (H // 2)])
+        pick_words(0)
+        w1_raw = over.tile([PARTS, PASSES, 2, PACK, H // 2], F32, name="w1_raw", offset=4 * BANK, align_bytes=64)
+        for a in range(PASSES):
+            for c in range(2):
+                nc.sync.dma_start(w1_raw[:, a, c], w1_rows[a][:, :, c * (H // 2) : (c + 1) * (H // 2)])
+        w2_plane = held([PARTS, PASSES, PACK, 128], U8, "w2_plane")
+        nc.gpsimd.tensor_copy(w2_plane[:], w2_scales_raw[:].rearrange("p a (m t) -> p a t m", t=PACK))
         pick_words(1)
         wash_t = held([PARTS, PACK, P], F32, "wash_t", "slot_a")
         nc.sync.dma_start(wash_t[:], wash.rearrange("(p t) j -> p t j", t=PACK))
 
-        linear = [held([PARTS, S], F32, f"linear{t}") for t in range(PACK)]
-
-        def linear_part(unit):
-            t, hf = divmod(unit, 2)
-            cols = slice(hf * BANK, (hf + 1) * BANK)
-            e2 = psum.tile([PARTS, BANK], F32, name="e2", tag="bank")
-            for a in range(PASSES):
-                nc.tensor.matmul_mx(
-                    e2[:], w2_codes[:, a, 256 * t : 256 * (t + 1)].bitcast(E2M1), w2_plane[:, a, t, :],
-                    picked[a][hf][:].bitcast(E4M3), picked_plane[a][:, cols],
-                    start=(a == 0), stop=(a == PASSES - 1),
-                )
-            nc.scalar.activation(linear[t][:, cols], e2[:], ACT.Copy, scale=gain_t[:, t : t + 1])
-
-        for unit in range(LINEAR_AHEAD):
-            linear_part(unit)
-
         w1_bf = [held([PARTS, PACK, 128, PACK], BF16, f"w1_bf{a}", ("slot_b", "slot_f")[a]) for a in range(PASSES)]
         w1_codes = [held([PARTS, H], U32, f"w1_codes{a}") for a in range(PASSES)]
         w1_plane = [held([PARTS, H], U8, f"w1_plane{a}") for a in range(PASSES)]
-        nc.vector.tensor_copy(
-            w1_bf[0][:].rearrange("p t m j -> p m t j"),
-            w1_raw0[:].rearrange("p j (m t) -> p m t j", t=PACK),
-        )
+
+        def weave_w1(a, c):
+            copy = nc.scalar.copy if a == 0 else nc.vector.tensor_copy
+            copy(
+                w1_bf[a][:, :, c * 64 : (c + 1) * 64, :].rearrange("p t m j -> p m t j"),
+                w1_raw[:, a, c].rearrange("p j (m t) -> p m t j", t=PACK),
+            )
+
+        for c in range(2):
+            weave_w1(0, c)
         nc.vector.quantize_mx(
             w1_codes[0][:].bitcast(E4M3), w1_plane[0][:], w1_bf[0][:].rearrange("p t m j -> p (t m j)")
         )
         for c in range(2):
-            nc.vector.tensor_copy(
-                w1_bf[1][:, :, c * 64 : (c + 1) * 64, :].rearrange("p t m j -> p m t j"),
-                w1_raw1[:, c].rearrange("p j (m t) -> p m t j", t=PACK),
-            )
+            weave_w1(1, c)
         w1_flat = w1_bf[1][:].rearrange("p t m j -> p (t m j)")
         for lo, hi in ((0, 128), (128, H)):
             nc.vector.quantize_mx(
@@ -155,9 +140,9 @@ def tile_list_hair_segment_readings_kernel(
             )
 
         w3_rows = w3.rearrange("(p t) n -> p t n", t=PACK)
-        w3_raw = [held([PARTS, PACK, N // 2], F32, f"w3_raw{c}", ("slot_d", "slot_c")[c]) for c in range(2)]
+        w3_raw = over.tile([PARTS, 2, PACK, N // 2], F32, name="w3_raw", offset=4 * BANK, align_bytes=64)
         for c in range(2):
-            nc.sync.dma_start(w3_raw[c][:], w3_rows[:, :, c * (N // 2) : (c + 1) * (N // 2)])
+            nc.sync.dma_start(w3_raw[:, c], w3_rows[:, :, c * (N // 2) : (c + 1) * (N // 2)])
         w4_codes = held([PARTS, 2 * N], U8, "w4_codes", "slot_b")
         nc.sync.dma_start(w4_codes[:].bitcast(I32), w4_words[0].bitcast(I32))
 
@@ -166,7 +151,6 @@ def tile_list_hair_segment_readings_kernel(
         xb = held([PARTS, P, PACK], BF16, "xb")
         xa_low = held([PARTS, 2, P], BF16, "xa_low")
         xb_f32 = [held([PARTS, 2, P], F32, f"xb_f32{u}") for u in range(2)]
-        near = [held([PARTS, P], F32, f"near{t}") for t in range(PACK)]
         w3_bf = held([PARTS, N, PACK], BF16, "w3_bf")
         w3_codes = held([PARTS, N], U32, "w3_codes")
         w3_plane = held([PARTS, N], U8, "w3_plane")
@@ -174,47 +158,54 @@ def tile_list_hair_segment_readings_kernel(
         def features(t, hf):
             cols = slice(hf * BANK, (hf + 1) * BANK)
             rows = slice(t * 128, (t + 1) * 128)
-            e1 = psum.tile([PARTS, BANK], F32, name="e1", tag="bank")
+            e1 = psum.tile([PARTS, BANK], F32, name="e1", tag="first", bufs=5)
+            e2 = psum.tile([PARTS, BANK], F32, name="e2", tag="second", bufs=3)
             for a in range(PASSES):
                 nc.tensor.matmul_mx(
                     e1[:], w1_codes[a][:, rows].bitcast(E4M3), w1_plane[a][:, rows],
-                    picked[a][hf][:].bitcast(E4M3), picked_plane[a][:, cols],
+                    picked[a][hf][:].bitcast(E4M3), picked_scales[4 * a :, cols],
+                    start=(a == 0), stop=(a == PASSES - 1),
+                )
+            for a, plane in enumerate((picked_scales, moved_scales)):
+                nc.tensor.matmul_mx(
+                    e2[:], w2_codes[:, a, 256 * t : 256 * (t + 1)].bitcast(E2M1), w2_plane[:, a, t, :],
+                    picked[a][hf][:].bitcast(E4M3), plane[:, cols],
                     start=(a == 0), stop=(a == PASSES - 1),
                 )
             turns = work.tile([PARTS, BANK], F32, name="turns")
-            whole = work.tile([PARTS, BANK], I32, name="whole")
+            whole = work.tile([PARTS, BANK], U32, name="whole")
             rest = work.tile([PARTS, BANK], F32, name="rest")
-            if hf == 0 and t > 0:
-                cosine = near[t - 1]
-                wave = xb_f32[(t - 1) // 2][:, (t - 1) % 2, :]
-            else:
-                cosine = work.tile([PARTS, BANK], F32, name="cosine")
-                wave_tile = work.tile([PARTS, BANK], F32, name="wave_tile")
-                wave = wave_tile[:]
+            cosine = work.tile([PARTS, BANK], F32, name="cosine")
+            wave = work.tile([PARTS, BANK], F32, name="wave")
             nc.scalar.activation(turns[:], e1[:], ACT.Copy, bias=0.25, scale=1.0 / (2.0 * math.pi))
-            nc.gpsimd.tensor_scalar(whole[:], turns[:], 1.0, 0.0, ALU.mult, ALU.add)
-            nc.vector.scalar_tensor_tensor(rest[:], whole[:], -2.0 * math.pi, e1[:], ALU.mult, ALU.add)
-            nc.scalar.activation(cosine[:], rest[:], ACT.Sin, bias=math.pi / 2.0, scale=1.0)
-            nc.vector.scalar_tensor_tensor(wave, cosine[:], gain_t[:, t : t + 1], e1[:], ALU.mult, ALU.mult)
-            nc.gpsimd.tensor_tensor(h[t][:, cols], wave, linear[t][:, cols], ALU.add)
+            nc.scalar.activation(whole[:], turns[:], ACT.Copy, bias=ROUNDER, scale=1.0)
+            nc.vector.scalar_tensor_tensor(
+                rest[:], whole[:].bitcast(I32), ROUNDER, turns[:], ALU.subtract, ALU.subtract
+            )
+            nc.scalar.activation(cosine[:], rest[:], ACT.Sin, scale=-2.0 * math.pi)
+            nc.vector.scalar_tensor_tensor(wave[:], cosine[:], gain_t[:, t : t + 1], e1[:], ALU.mult, ALU.mult)
+            nc.vector.scalar_tensor_tensor(h[t][:, cols], e2[:], gain_t[:, t : t + 1], wave[:], ALU.mult, ALU.add)
 
         def pick(t, lo, hi):
             entries = slice(lo // 16, hi // 16)
-            nc.vector.tensor_copy(near[t][:, lo:hi], h[t][:].indirect(pos1_t[:, entries]))
-            target = xa_low[:, t, lo:hi] if t < 2 else xa[:, lo:hi, t]
             nc.vector.tensor_tensor(
                 xb_f32[t // 2][:, t % 2, lo:hi], h[t][:].indirect(pos2_t[:, entries]), wash_t[:, t, lo:hi], ALU.add
             )
-            nc.vector.tensor_scalar_max(target, near[t][:, lo:hi], base_t[:, t : t + 1])
+            near = work.tile([PARTS, hi - lo], F32, name="near")
+            nc.vector.tensor_copy(near[:], h[t][:].indirect(pos1_t[:, entries]))
+            target = xa_low[:, t, lo:hi] if t < 2 else xa[:, lo:hi, t]
+            nc.vector.tensor_scalar_max(target, near[:], base_t[:, t : t + 1])
 
         def weave_xb(u, lo, hi):
             nc.scalar.copy(xb[:, lo:hi, 2 * u : 2 * u + 2], xb_f32[u][:, :, lo:hi].rearrange("p t j -> p j t"))
 
         def weave_w3(c):
-            nc.scalar.copy(
-                w3_bf[:, c * (N // 2) : (c + 1) * (N // 2), :].rearrange("p (g i) t -> p g t i", i=4),
-                w3_raw[c][:].rearrange("p t (g i) -> p g t i", i=4),
-            )
+            for lo in (0, N // 4):
+                n0 = c * (N // 2) + lo
+                nc.scalar.copy(
+                    w3_bf[:, n0 : n0 + N // 4, :].rearrange("p (g i) t -> p g t i", i=4),
+                    w3_raw[:, c, :, lo : lo + N // 4].rearrange("p t (g i) -> p g t i", i=4),
+                )
 
         def quantise_w3(c):
             cols = slice(c * (N // 2), (c + 1) * (N // 2))
@@ -225,8 +216,6 @@ def tile_list_hair_segment_readings_kernel(
         for t in range(PACK):
             for hf in range(2):
                 features(t, hf)
-                if 2 * t + hf + LINEAR_AHEAD < 2 * PACK:
-                    linear_part(2 * t + hf + LINEAR_AHEAD)
             if t >= 1:
                 pick(t - 1, 0, P)
             if t == 2:
@@ -244,7 +233,6 @@ def tile_list_hair_segment_readings_kernel(
         for hf in range(2):
             pick(PACK - 1, hf * HALF, (hf + 1) * HALF)
             weave_xb(1, hf * HALF, (hf + 1) * HALF)
-        for hf in range(2):
             cols = slice(hf * HALF, (hf + 1) * HALF)
             for codes, plane, x in ((xa_codes, xa_plane, xa), (xb_codes, xb_plane, xb)):
                 nc.vector.quantize_mx(
@@ -253,8 +241,8 @@ def tile_list_hair_segment_readings_kernel(
         for hf in range(2):
             cols = slice(hf * HALF, (hf + 1) * HALF)
             for pair in range(N // 256):
-                ya = psum.tile([PARTS, 2, HALF], F32, name="ya", tag="bank")
-                yb = psum.tile([PARTS, 2, HALF], F32, name="yb", tag="bank")
+                ya = psum.tile([PARTS, 2, HALF], F32, name="ya", tag="first", bufs=5)
+                yb = psum.tile([PARTS, 2, HALF], F32, name="yb", tag="second", bufs=3)
                 for i in range(2):
                     n0 = (2 * pair + i) * 128
                     nc.tensor.matmul_mx(

@@ -22,7 +22,9 @@ PACK = 4
 PASSES = K // 512
 BANK = 512
 HALF = P // 2
-ROUNDER = 1.5 * 2.0**23
+LINEAR_AHEAD = 3
+COS_AT = {1: 6144, 2: 8192, 3: 3072}
+NEAR_AT = {0: 6144, 1: 8192, 2: 4096, 3: 10240}
 
 
 def tile_list_hair_segment_readings_kernel(
@@ -34,6 +36,7 @@ def tile_list_hair_segment_readings_kernel(
         keep = ctx.enter_context(tc.tile_pool(name="keep", bufs=1))
         work = ctx.enter_context(tc.tile_pool(name="work", bufs=4))
         over = ctx.enter_context(tc.tile_pool(name="over", bufs=1))
+        late = ctx.enter_context(tc.tile_pool(name="late", bufs=1))
         psum = ctx.enter_context(tc.psum_pool(name="psum", bufs=1))
 
         def held(shape, dtype, name, tag=None):
@@ -43,16 +46,15 @@ def tile_list_hair_segment_readings_kernel(
         pos1_t = held([PARTS, P // 16], U16, "pos1_t")
         pos2_t = held([PARTS, P // 16], U16, "pos2_t")
         table0 = held([PARTS, T], U32, "table0")
-        table_scales = over.tile([PARTS, T], U8, name="table_scales", offset=0, align_bytes=64)
+        table_scales = over.tile([PARTS, T], U8, name="table_scales", offset=1024, align_bytes=64)
         w2_raw = [held([PARTS, 2 * H], U8, f"w2_raw{a}", ("slot_a", "slot_e")[a]) for a in range(PASSES)]
-        w4_plane = held([PARTS, N], U8, "w4_plane")
         gain_t = held([PARTS, PACK], F32, "gain_t")
-        base_t = held([PARTS, PACK], F32, "base_t")
+        w2_scales_raw = held([PARTS, PASSES, H], U8, "w2_scales_raw")
         moved_scales = held([PARTS, S], U8, "moved_scales")
 
         nc.vector.memset(table_scales[:].bitcast(I32), 0)
         nc.vector.memset(moved_scales[:].bitcast(I32), 0)
-        nc.gpsimd.memset(w4_plane[:].bitcast(I32), 0)
+        nc.gpsimd.memset(w2_scales_raw[:].bitcast(I32), 0)
         nc.sync.dma_start(offs_t[:], offs)
         for a in range(PASSES):
             nc.sync.dma_start(w2_raw[a][:].bitcast(I32), w2_words[a].bitcast(I32))
@@ -74,24 +76,18 @@ def tile_list_hair_segment_readings_kernel(
         table1 = held([PARTS, T], U32, "table1", "slot_a")
         nc.sync.dma_start(table1[:].bitcast(I32), tab_words[1].rearrange("p t i -> p (t i)").bitcast(I32))
         table = [table0, table1]
-        w2_scales_raw = held([PARTS, PASSES, H], U8, "w2_scales_raw", "slot_e")
-        nc.vector.memset(w2_scales_raw[:].bitcast(I32), 0)
-        for q in range(4):
-            nc.sync.dma_start(
-                w2_scales_raw[32 * q : 32 * q + 4, :, :].bitcast(I32),
-                w2_scales[:, 4 * q : 4 * q + 4, :].rearrange("a r c -> r a c").bitcast(I32),
-            )
+        base_t = held([PARTS, PACK], F32, "base_t", "slot_e")
+        nc.sync.dma_start(base_t[:], base.rearrange("(p t) -> p t", t=PACK))
         nc.gpsimd.dma_start(gain_t[:], gain.rearrange("(p t) -> p t", t=PACK))
-        nc.gpsimd.dma_start(base_t[:], base.rearrange("(p t) -> p t", t=PACK))
         for q in range(4):
             nc.gpsimd.dma_start(
-                w4_plane[32 * q : 32 * q + 4, :].bitcast(I32),
-                w4_scales[0, 4 * q : 4 * q + 4, :].bitcast(I32),
+                w2_scales_raw[32 * q : 32 * q + 4, :, :].bitcast(I32),
+                w2_scales[:, 4 * q : 4 * q + 4, :].rearrange("a r c -> r a c").bitcast(I32),
             )
         w1_rows = w1.rearrange("(a p j) c -> a p j c", a=PASSES, j=PACK)
 
         picked = [
-            [held([PARTS, BANK], U32, "picked00"), over.tile([PARTS, BANK], U32, name="picked01", offset=0, align_bytes=64)],
+            [over.tile([PARTS, BANK], U32, name=f"picked0{hf}", offset=2048 * hf, align_bytes=64) for hf in range(2)],
             [held([PARTS, BANK], U32, "picked10"), held([PARTS, BANK], U32, "picked11")],
         ]
 
@@ -103,128 +99,157 @@ def tile_list_hair_segment_readings_kernel(
 
         picked_scales = held([PARTS, S], U8, "picked_scales")
         nc.vector.tensor_copy(picked_scales[:], table_scales[:].indirect(offs_t[:]))
-        nc.scalar.dma_start(moved_scales[0:112, :].bitcast(I32), picked_scales[4:116, :].bitcast(I32))
+        for q in range(4):
+            nc.sync.dma_start(
+                moved_scales[32 * q : 32 * q + 4, :].bitcast(I32),
+                picked_scales[32 * q + 4 : 32 * q + 8, :].bitcast(I32),
+            )
         pick_words(0)
-        w1_raw = over.tile([PARTS, PASSES, 2, PACK, H // 2], F32, name="w1_raw", offset=4 * BANK, align_bytes=64)
+        w1_raw = over.tile([PARTS, PASSES, PACK, H], F32, name="w1_raw", offset=4096, align_bytes=64)
         for a in range(PASSES):
-            for c in range(2):
-                nc.sync.dma_start(w1_raw[:, a, c], w1_rows[a][:, :, c * (H // 2) : (c + 1) * (H // 2)])
+            nc.sync.dma_start(w1_raw[:, a], w1_rows[a])
         w2_plane = held([PARTS, PASSES, PACK, 128], U8, "w2_plane")
         nc.gpsimd.tensor_copy(w2_plane[:], w2_scales_raw[:].rearrange("p a (m t) -> p a t m", t=PACK))
         pick_words(1)
         wash_t = held([PARTS, PACK, P], F32, "wash_t", "slot_a")
         nc.sync.dma_start(wash_t[:], wash.rearrange("(p t) j -> p t j", t=PACK))
 
-        w1_bf = [held([PARTS, PACK, 128, PACK], BF16, f"w1_bf{a}", ("slot_b", "slot_f")[a]) for a in range(PASSES)]
-        w1_codes = [held([PARTS, H], U32, f"w1_codes{a}") for a in range(PASSES)]
-        w1_plane = [held([PARTS, H], U8, f"w1_plane{a}") for a in range(PASSES)]
+        linear = [held([PARTS, S], F32, f"linear{t}") for t in range(PACK)]
 
-        def weave_w1(a, c):
-            copy = nc.scalar.copy if a == 0 else nc.vector.tensor_copy
-            copy(
-                w1_bf[a][:, :, c * 64 : (c + 1) * 64, :].rearrange("p t m j -> p m t j"),
-                w1_raw[:, a, c].rearrange("p j (m t) -> p m t j", t=PACK),
-            )
+        def bank(name, number, shape):
+            return psum.tile(shape, F32, name=name, tag=f"bank{number}")
 
-        for c in range(2):
-            weave_w1(0, c)
-        nc.vector.quantize_mx(
-            w1_codes[0][:].bitcast(E4M3), w1_plane[0][:], w1_bf[0][:].rearrange("p t m j -> p (t m j)")
-        )
-        for c in range(2):
-            weave_w1(1, c)
-        w1_flat = w1_bf[1][:].rearrange("p t m j -> p (t m j)")
-        for lo, hi in ((0, 128), (128, H)):
-            nc.vector.quantize_mx(
-                w1_codes[1][:, lo:hi].bitcast(E4M3), w1_plane[1][:, lo:hi], w1_flat[:, PACK * lo : PACK * hi]
-            )
-
-        w3_rows = w3.rearrange("(p t) n -> p t n", t=PACK)
-        w3_raw = over.tile([PARTS, 2, PACK, N // 2], F32, name="w3_raw", offset=4 * BANK, align_bytes=64)
-        for c in range(2):
-            nc.sync.dma_start(w3_raw[:, c], w3_rows[:, :, c * (N // 2) : (c + 1) * (N // 2)])
-        w4_codes = held([PARTS, 2 * N], U8, "w4_codes", "slot_b")
-        nc.sync.dma_start(w4_codes[:].bitcast(I32), w4_words[0].bitcast(I32))
-
-        h = [held([PARTS, S], F32, f"h{t}") for t in range(PACK)]
-        xa = held([PARTS, P, PACK], BF16, "xa")
-        xb = held([PARTS, P, PACK], BF16, "xb")
-        xa_low = held([PARTS, 2, P], BF16, "xa_low")
-        xb_f32 = [held([PARTS, 2, P], F32, f"xb_f32{u}") for u in range(2)]
-        w3_bf = held([PARTS, N, PACK], BF16, "w3_bf")
-        w3_codes = held([PARTS, N], U32, "w3_codes")
-        w3_plane = held([PARTS, N], U8, "w3_plane")
-
-        def features(t, hf):
+        def linear_part(unit):
+            t, hf = divmod(unit, 2)
             cols = slice(hf * BANK, (hf + 1) * BANK)
-            rows = slice(t * 128, (t + 1) * 128)
-            e1 = psum.tile([PARTS, BANK], F32, name="e1", tag="first", bufs=5)
-            e2 = psum.tile([PARTS, BANK], F32, name="e2", tag="second", bufs=3)
-            for a in range(PASSES):
-                nc.tensor.matmul_mx(
-                    e1[:], w1_codes[a][:, rows].bitcast(E4M3), w1_plane[a][:, rows],
-                    picked[a][hf][:].bitcast(E4M3), picked_scales[4 * a :, cols],
-                    start=(a == 0), stop=(a == PASSES - 1),
-                )
+            e2 = bank("e2", unit, [PARTS, BANK])
             for a, plane in enumerate((picked_scales, moved_scales)):
                 nc.tensor.matmul_mx(
                     e2[:], w2_codes[:, a, 256 * t : 256 * (t + 1)].bitcast(E2M1), w2_plane[:, a, t, :],
                     picked[a][hf][:].bitcast(E4M3), plane[:, cols],
                     start=(a == 0), stop=(a == PASSES - 1),
                 )
-            turns = work.tile([PARTS, BANK], F32, name="turns")
-            whole = work.tile([PARTS, BANK], U32, name="whole")
-            rest = work.tile([PARTS, BANK], F32, name="rest")
-            cosine = work.tile([PARTS, BANK], F32, name="cosine")
-            wave = work.tile([PARTS, BANK], F32, name="wave")
-            nc.scalar.activation(turns[:], e1[:], ACT.Copy, bias=0.25, scale=1.0 / (2.0 * math.pi))
-            nc.scalar.activation(whole[:], turns[:], ACT.Copy, bias=ROUNDER, scale=1.0)
-            nc.vector.scalar_tensor_tensor(
-                rest[:], whole[:].bitcast(I32), ROUNDER, turns[:], ALU.subtract, ALU.subtract
+            nc.scalar.activation(linear[t][:, cols], e2[:], ACT.Copy, scale=gain_t[:, t : t + 1])
+
+        for unit in range(LINEAR_AHEAD):
+            linear_part(unit)
+
+        w1_bf = [held([PARTS, PACK, 128, PACK], BF16, f"w1_bf{a}", ("slot_b", "slot_f")[a]) for a in range(PASSES)]
+        w1_codes = [held([PARTS, H], U32, f"w1_codes{a}") for a in range(PASSES)]
+        w1_plane = [held([PARTS, H], U8, f"w1_plane{a}") for a in range(PASSES)]
+
+        def weave_w1(copy, a, lo, hi):
+            copy(
+                w1_bf[a][:, lo:hi].rearrange("p t m j -> p m t j"),
+                w1_raw[:, a].rearrange("p j (m t) -> p m t j", t=PACK)[:, :, lo:hi, :],
             )
-            nc.scalar.activation(cosine[:], rest[:], ACT.Sin, scale=-2.0 * math.pi)
-            nc.vector.scalar_tensor_tensor(wave[:], cosine[:], gain_t[:, t : t + 1], e1[:], ALU.mult, ALU.mult)
-            nc.vector.scalar_tensor_tensor(h[t][:, cols], e2[:], gain_t[:, t : t + 1], wave[:], ALU.mult, ALU.add)
+
+        def quantise_w1(a, lo, hi):
+            cols = slice(128 * lo, 128 * hi)
+            nc.vector.quantize_mx(
+                w1_codes[a][:, cols].bitcast(E4M3), w1_plane[a][:, cols],
+                w1_bf[a][:, lo:hi].rearrange("p t m j -> p (t m j)"),
+            )
+
+        weave_w1(nc.vector.tensor_copy, 0, 0, PACK)
+        quantise_w1(0, 0, PACK)
+        weave_w1(nc.vector.tensor_copy, 1, 0, 2)
+        weave_w1(nc.scalar.copy, 1, 2, PACK)
+        quantise_w1(1, 0, 1)
+        quantise_w1(1, 1, 2)
+        quantise_w1(1, 2, PACK)
+
+        w3_rows = w3.rearrange("(p t) n -> p t n", t=PACK)
+        w3_raw = over.tile([PARTS, PACK, N], F32, name="w3_raw", offset=4096, align_bytes=64)
+        nc.sync.dma_start(w3_raw[:], w3_rows)
+        w4_codes = held([PARTS, 2 * N], U8, "w4_codes", "slot_b")
+        nc.sync.dma_start(w4_codes[:].bitcast(I32), w4_words[0].bitcast(I32))
+        w4_plane = held([PARTS, N], U8, "w4_plane", "slot_f")
+        nc.gpsimd.memset(w4_plane[:].bitcast(I32), 0)
+        for q in range(4):
+            nc.sync.dma_start(
+                w4_plane[32 * q : 32 * q + 4, :].bitcast(I32),
+                w4_scales[0, 4 * q : 4 * q + 4, :].bitcast(I32),
+            )
+
+        h = [held([PARTS, S], F32, f"h{t}") for t in range(PACK)]
+        xa_low = held([PARTS, 2, P], BF16, "xa_low")
+        xb_f32 = [held([PARTS, 2, P], F32, f"xb_f32{u}") for u in range(2)]
+        w3_codes = held([PARTS, N], U32, "w3_codes")
+        w3_plane = held([PARTS, N], U8, "w3_plane")
+
+        def features(t, hf):
+            cols = slice(hf * BANK, (hf + 1) * BANK)
+            rows = slice(t * 128, (t + 1) * 128)
+            e1 = bank("e1", (2 * t + hf + 3) % 8, [PARTS, BANK])
+            for a in range(PASSES):
+                nc.tensor.matmul_mx(
+                    e1[:], w1_codes[a][:, rows].bitcast(E4M3), w1_plane[a][:, rows],
+                    picked[a][hf][:].bitcast(E4M3), picked_scales[4 * a :, cols],
+                    start=(a == 0), stop=(a == PASSES - 1),
+                )
+            turns = work.tile([PARTS, BANK], F32, name="turns")
+            whole = work.tile([PARTS, BANK], I32, name="whole")
+            if hf == 0 and t > 0:
+                rest = held([PARTS, BANK], F32, f"rest{t}", f"after_sin{t}")
+                cosine = late.tile([PARTS, BANK], F32, name=f"cosine{t}", offset=COS_AT[t], align_bytes=64)
+                wave = xb_f32[(t - 1) // 2][:, (t - 1) % 2, :]
+            else:
+                rest = work.tile([PARTS, BANK], F32, name="rest")
+                cosine = work.tile([PARTS, BANK], F32, name="cosine")
+                wave_tile = work.tile([PARTS, BANK], F32, name="wave_tile")
+                wave = wave_tile[:]
+            nc.scalar.activation(turns[:], e1[:], ACT.Copy, bias=0.25, scale=1.0 / (2.0 * math.pi))
+            nc.gpsimd.tensor_scalar(whole[:], turns[:], 1.0, 0.0, ALU.mult, ALU.add)
+            nc.vector.scalar_tensor_tensor(rest[:], whole[:], -2.0 * math.pi, e1[:], ALU.mult, ALU.add)
+            nc.scalar.activation(cosine[:], rest[:], ACT.Sin, bias=math.pi / 2.0, scale=1.0)
+            nc.vector.scalar_tensor_tensor(wave, cosine[:], gain_t[:, t : t + 1], e1[:], ALU.mult, ALU.mult)
+            if 2 * t + hf + LINEAR_AHEAD < 2 * PACK:
+                linear_part(2 * t + hf + LINEAR_AHEAD)
+            adder = nc.vector if 2 * t + hf == 2 * PACK - 1 else nc.gpsimd
+            adder.tensor_tensor(h[t][:, cols], wave, linear[t][:, cols], ALU.add)
+
+        near = {}
 
         def pick(t, lo, hi):
             entries = slice(lo // 16, hi // 16)
+            if t not in near:
+                near[t] = late.tile([PARTS, P], F32, name=f"near{t}", offset=NEAR_AT[t], align_bytes=64)
             nc.vector.tensor_tensor(
                 xb_f32[t // 2][:, t % 2, lo:hi], h[t][:].indirect(pos2_t[:, entries]), wash_t[:, t, lo:hi], ALU.add
             )
-            near = work.tile([PARTS, hi - lo], F32, name="near")
-            nc.vector.tensor_copy(near[:], h[t][:].indirect(pos1_t[:, entries]))
+            nc.vector.tensor_copy(near[t][:, lo:hi], h[t][:].indirect(pos1_t[:, entries]))
             target = xa_low[:, t, lo:hi] if t < 2 else xa[:, lo:hi, t]
-            nc.vector.tensor_scalar_max(target, near[:], base_t[:, t : t + 1])
+            nc.vector.tensor_scalar_max(target, near[t][:, lo:hi], base_t[:, t : t + 1])
 
         def weave_xb(u, lo, hi):
             nc.scalar.copy(xb[:, lo:hi, 2 * u : 2 * u + 2], xb_f32[u][:, :, lo:hi].rearrange("p t j -> p j t"))
 
-        def weave_w3(c):
+        def prepare_w3(c):
+            w3_bf = held([PARTS, N // 2, PACK], BF16, f"w3_bf{c}", f"after_sin{c + 1}")
             for lo in (0, N // 4):
                 n0 = c * (N // 2) + lo
                 nc.scalar.copy(
-                    w3_bf[:, n0 : n0 + N // 4, :].rearrange("p (g i) t -> p g t i", i=4),
-                    w3_raw[:, c, :, lo : lo + N // 4].rearrange("p t (g i) -> p g t i", i=4),
+                    w3_bf[:, lo : lo + N // 4, :].rearrange("p (g i) t -> p g t i", i=4),
+                    w3_raw[:, :, n0 : n0 + N // 4].rearrange("p t (g i) -> p g t i", i=4),
                 )
-
-        def quantise_w3(c):
             cols = slice(c * (N // 2), (c + 1) * (N // 2))
             nc.vector.quantize_mx(
-                w3_codes[:, cols].bitcast(E4M3), w3_plane[:, cols], w3_bf[:, cols, :].rearrange("p n t -> p (n t)")
+                w3_codes[:, cols].bitcast(E4M3), w3_plane[:, cols], w3_bf[:].rearrange("p n t -> p (n t)")
             )
 
         for t in range(PACK):
             for hf in range(2):
                 features(t, hf)
+            if t == PACK - 1:
+                xa = late.tile([PARTS, P, PACK], BF16, name="xa", offset=0, align_bytes=64)
+                xb = held([PARTS, P, PACK], BF16, "xb", f"after_sin{t}")
             if t >= 1:
                 pick(t - 1, 0, P)
-            if t == 2:
-                nc.scalar.copy(xa[:, :, 0:2], xa_low[:].rearrange("p t j -> p j t"))
-                weave_xb(0, 0, P)
             if t in (1, 2):
-                weave_w3(t - 1)
-            if t >= 2:
-                quantise_w3(t - 2)
+                prepare_w3(t - 1)
+        weave_xb(0, 0, P)
+        nc.scalar.copy(xa[:, :, 0:2], xa_low[:].rearrange("p t j -> p j t"))
 
         xa_codes = held([PARTS, P], U32, "xa_codes")
         xb_codes = held([PARTS, P], U32, "xb_codes")
@@ -241,8 +266,8 @@ def tile_list_hair_segment_readings_kernel(
         for hf in range(2):
             cols = slice(hf * HALF, (hf + 1) * HALF)
             for pair in range(N // 256):
-                ya = psum.tile([PARTS, 2, HALF], F32, name="ya", tag="first", bufs=5)
-                yb = psum.tile([PARTS, 2, HALF], F32, name="yb", tag="second", bufs=3)
+                ya = bank("ya", (3 + 2 * (3 * hf + pair)) % 8, [PARTS, 2, HALF])
+                yb = bank("yb", (4 + 2 * (3 * hf + pair)) % 8, [PARTS, 2, HALF])
                 for i in range(2):
                     n0 = (2 * pair + i) * 128
                     nc.tensor.matmul_mx(

@@ -45,25 +45,23 @@ def tile_list_hair_segment_readings_kernel(
         offs_t = held([PARTS, S // 16], U16, "offs_t")
         pos1_t = held([PARTS, P // 16], U16, "pos1_t")
         pos2_t = held([PARTS, P // 16], U16, "pos2_t")
-        table0 = held([PARTS, T], U32, "table0")
-        table_scales = over.tile([PARTS, T], U8, name="table_scales", offset=1024, align_bytes=64)
+        table0 = held([PARTS, T], U32, "table0", "slot_d")
+        table_scales = over.tile([PARTS, T], U8, name="table_scales", offset=0, align_bytes=64)
         w2_raw = [held([PARTS, 2 * H], U8, f"w2_raw{a}", ("slot_a", "slot_e")[a]) for a in range(PASSES)]
         gain_t = held([PARTS, PACK], F32, "gain_t")
         w2_scales_raw = held([PARTS, PASSES, H], U8, "w2_scales_raw")
-        moved_scales = held([PARTS, S], U8, "moved_scales")
+        picked_plane = held([PARTS, PASSES, S], U8, "picked_plane")
 
         nc.vector.memset(table_scales[:].bitcast(I32), 0)
-        nc.vector.memset(moved_scales[:].bitcast(I32), 0)
+        nc.vector.memset(picked_plane[:].bitcast(I32), 0)
         nc.gpsimd.memset(w2_scales_raw[:].bitcast(I32), 0)
         nc.sync.dma_start(offs_t[:], offs)
         for a in range(PASSES):
             nc.sync.dma_start(w2_raw[a][:].bitcast(I32), w2_words[a].bitcast(I32))
         nc.sync.dma_start(table0[:].bitcast(I32), tab_words[0].rearrange("p t i -> p (t i)").bitcast(I32))
-        for q in range(4):
-            nc.sync.dma_start(
-                table_scales[32 * q : 32 * q + 8, :].bitcast(I32),
-                tab_scales[:, 4 * q : 4 * q + 4, :].bitcast(I32),
-            )
+        nc.scalar.dma_start(
+            table_scales[0:PARTS:4, :].bitcast(I32), tab_scales.rearrange("a q t -> (a q) t").bitcast(I32)
+        )
         nc.sync.dma_start(pos1_t[:], pos1)
         nc.sync.dma_start(pos2_t[:], pos2)
 
@@ -76,15 +74,18 @@ def tile_list_hair_segment_readings_kernel(
         table1 = held([PARTS, T], U32, "table1", "slot_a")
         nc.sync.dma_start(table1[:].bitcast(I32), tab_words[1].rearrange("p t i -> p (t i)").bitcast(I32))
         table = [table0, table1]
-        base_t = held([PARTS, PACK], F32, "base_t", "slot_e")
-        nc.sync.dma_start(base_t[:], base.rearrange("(p t) -> p t", t=PACK))
+        w1_rows = w1.rearrange("(a p j) c -> a p j c", a=PASSES, j=PACK)
+        w1_raw = held([PARTS, PASSES, PACK, H], F32, "w1_raw", "slot_e")
+        for a in range(PASSES):
+            nc.sync.dma_start(w1_raw[:, a], w1_rows[a])
+        base_t = held([PARTS, PACK], F32, "base_t")
         nc.gpsimd.dma_start(gain_t[:], gain.rearrange("(p t) -> p t", t=PACK))
         for q in range(4):
             nc.gpsimd.dma_start(
                 w2_scales_raw[32 * q : 32 * q + 4, :, :].bitcast(I32),
                 w2_scales[:, 4 * q : 4 * q + 4, :].rearrange("a r c -> r a c").bitcast(I32),
             )
-        w1_rows = w1.rearrange("(a p j) c -> a p j c", a=PASSES, j=PACK)
+        nc.gpsimd.dma_start(base_t[:], base.rearrange("(p t) -> p t", t=PACK))
 
         picked = [
             [over.tile([PARTS, BANK], U32, name=f"picked0{hf}", offset=2048 * hf, align_bytes=64) for hf in range(2)],
@@ -99,17 +100,16 @@ def tile_list_hair_segment_readings_kernel(
 
         picked_scales = held([PARTS, S], U8, "picked_scales")
         nc.vector.tensor_copy(picked_scales[:], table_scales[:].indirect(offs_t[:]))
-        for q in range(4):
-            nc.sync.dma_start(
-                moved_scales[32 * q : 32 * q + 4, :].bitcast(I32),
-                picked_scales[32 * q + 4 : 32 * q + 8, :].bitcast(I32),
-            )
-        pick_words(0)
-        w1_raw = over.tile([PARTS, PASSES, PACK, H], F32, name="w1_raw", offset=4096, align_bytes=64)
         for a in range(PASSES):
-            nc.sync.dma_start(w1_raw[:, a], w1_rows[a])
-        w2_plane = held([PARTS, PASSES, PACK, 128], U8, "w2_plane")
-        nc.gpsimd.tensor_copy(w2_plane[:], w2_scales_raw[:].rearrange("p a (m t) -> p a t m", t=PACK))
+            for q in range(4):
+                first = 64 * a + 16 * q
+                nc.scalar.dma_start(
+                    picked_plane[32 * q : 32 * q + 4, a, :].bitcast(I32),
+                    picked_scales[first : first + 16 : 4, :].bitcast(I32),
+                )
+        pick_words(0)
+        w2_plane = held([PARTS, PASSES, PACK, 128], U8, "w2_plane", "slot_d")
+        nc.vector.tensor_copy(w2_plane[:], w2_scales_raw[:].rearrange("p a (m t) -> p a t m", t=PACK))
         pick_words(1)
         wash_t = held([PARTS, PACK, P], F32, "wash_t", "slot_a")
         nc.sync.dma_start(wash_t[:], wash.rearrange("(p t) j -> p t j", t=PACK))
@@ -123,10 +123,10 @@ def tile_list_hair_segment_readings_kernel(
             t, hf = divmod(unit, 2)
             cols = slice(hf * BANK, (hf + 1) * BANK)
             e2 = bank("e2", unit, [PARTS, BANK])
-            for a, plane in enumerate((picked_scales, moved_scales)):
+            for a in range(PASSES):
                 nc.tensor.matmul_mx(
                     e2[:], w2_codes[:, a, 256 * t : 256 * (t + 1)].bitcast(E2M1), w2_plane[:, a, t, :],
-                    picked[a][hf][:].bitcast(E4M3), plane[:, cols],
+                    picked[a][hf][:].bitcast(E4M3), picked_plane[:, a, cols],
                     start=(a == 0), stop=(a == PASSES - 1),
                 )
             nc.scalar.activation(linear[t][:, cols], e2[:], ACT.Copy, scale=gain_t[:, t : t + 1])
@@ -160,7 +160,7 @@ def tile_list_hair_segment_readings_kernel(
         quantise_w1(1, 2, PACK)
 
         w3_rows = w3.rearrange("(p t) n -> p t n", t=PACK)
-        w3_raw = over.tile([PARTS, PACK, N], F32, name="w3_raw", offset=4096, align_bytes=64)
+        w3_raw = held([PARTS, PACK, N], F32, "w3_raw", "slot_e")
         nc.sync.dma_start(w3_raw[:], w3_rows)
         w4_codes = held([PARTS, 2 * N], U8, "w4_codes", "slot_b")
         nc.sync.dma_start(w4_codes[:].bitcast(I32), w4_words[0].bitcast(I32))
@@ -185,11 +185,11 @@ def tile_list_hair_segment_readings_kernel(
             for a in range(PASSES):
                 nc.tensor.matmul_mx(
                     e1[:], w1_codes[a][:, rows].bitcast(E4M3), w1_plane[a][:, rows],
-                    picked[a][hf][:].bitcast(E4M3), picked_scales[4 * a :, cols],
+                    picked[a][hf][:].bitcast(E4M3), picked_plane[:, a, cols],
                     start=(a == 0), stop=(a == PASSES - 1),
                 )
-            turns = work.tile([PARTS, BANK], F32, name="turns")
-            whole = work.tile([PARTS, BANK], I32, name="whole")
+            turns = work.tile([PARTS, BANK], F32, name="turns", bufs=2 * PACK)
+            whole = work.tile([PARTS, BANK], I32, name="whole", bufs=2 * PACK)
             if hf == 0 and t > 0:
                 rest = held([PARTS, BANK], F32, f"rest{t}", f"after_sin{t}")
                 cosine = late.tile([PARTS, BANK], F32, name=f"cosine{t}", offset=COS_AT[t], align_bytes=64)

import math
from contextlib import ExitStack

import concourse.mybir as mybir

K, T, S, P, H, N = 1024, 4096, 1024, 512, 512, 768
FLOPS = 2 * 2 * K * H * S + 2 * 2 * H * N * P

F32 = mybir.dt.float32
BF16 = mybir.dt.bfloat16
I32 = mybir.dt.int32
U32 = mybir.dt.uint32
U16 = mybir.dt.uint16
U8 = mybir.dt.uint8
E4M3 = mybir.dt.float8_e4m3fn_x4
E2M1 = mybir.dt.float4_e2m1fn_x4
ALU = mybir.AluOpType
ACT = mybir.ActivationFunctionType

PARTS = 128
PACK = 4
PASSES = K // 512
BANK = 512
HALF = P // 2
LINEAR_AHEAD = 3
COS_AT = {1: 6144, 2: 8192, 3: 3072}
NEAR_AT = {0: 6144, 1: 8192, 2: 4096, 3: 10240}


def tile_list_hair_segment_readings_kernel(
    tc, tab_words, tab_scales, offs, pos1, pos2, w1, w2_words, w2_scales,
    gain, base, wash, w3, w4_words, w4_scales, out,
):
    nc = tc.nc
    with ExitStack() as ctx:
        keep = ctx.enter_context(tc.tile_pool(name="keep", bufs=1))
        work = ctx.enter_context(tc.tile_pool(name="work", bufs=4))
        over = ctx.enter_context(tc.tile_pool(name="over", bufs=1))
        late = ctx.enter_context(tc.tile_pool(name="late", bufs=1))
        psum = ctx.enter_context(tc.psum_pool(name="psum", bufs=1))

        def held(shape, dtype, name, tag=None):
            return keep.tile(shape, dtype, name=name, tag=tag or name, align_bytes=64)

        offs_t = held([PARTS, S // 16], U16, "offs_t")
        pos1_t = held([PARTS, P // 16], U16, "pos1_t")
        pos2_t = held([PARTS, P // 16], U16, "pos2_t")
        table0 = held([PARTS, T], U32, "table0", "slot_d")
        table_scales = over.tile([PARTS, T], U8, name="table_scales", offset=0, align_bytes=64)
        w2_raw = [held([PARTS, 2 * H], U8, f"w2_raw{a}", ("slot_a", "slot_e")[a]) for a in range(PASSES)]
        gain_t = held([PARTS, PACK], F32, "gain_t")
        w2_scales_raw = held([PARTS, PASSES, H], U8, "w2_scales_raw")
        picked_plane = held([PARTS, PASSES, S], U8, "picked_plane")

        nc.vector.memset(table_scales[:].bitcast(I32), 0)
        nc.vector.memset(picked_plane[:].bitcast(I32), 0)
        nc.gpsimd.memset(w2_scales_raw[:].bitcast(I32), 0)
        nc.sync.dma_start(offs_t[:], offs)
        for a in range(PASSES):
            nc.sync.dma_start(w2_raw[a][:].bitcast(I32), w2_words[a].bitcast(I32))
        nc.sync.dma_start(table0[:].bitcast(I32), tab_words[0].rearrange("p t i -> p (t i)").bitcast(I32))
        nc.scalar.dma_start(
            table_scales[0:PARTS:4, :].bitcast(I32), tab_scales.rearrange("a q t -> (a q) t").bitcast(I32)
        )
        nc.sync.dma_start(pos1_t[:], pos1)
        nc.sync.dma_start(pos2_t[:], pos2)

        w2_codes = held([PARTS, PASSES, 2 * H], U8, "w2_codes")
        for a in range(PASSES):
            nc.vector.tensor_copy(
                w2_codes[:, a, :].rearrange("p (t m b) -> p t m b", t=PACK, b=2),
                w2_raw[a][:].rearrange("p (m t b) -> p t m b", t=PACK, b=2),
            )
        table1 = held([PARTS, T], U32, "table1", "slot_a")
        nc.sync.dma_start(table1[:].bitcast(I32), tab_words[1].rearrange("p t i -> p (t i)").bitcast(I32))
        table = [table0, table1]
        w1_rows = w1.rearrange("(a p j) c -> a p j c", a=PASSES, j=PACK)
        w1_raw = held([PARTS, PASSES, PACK, H], F32, "w1_raw", "slot_e")
        for a in range(PASSES):
            nc.sync.dma_start(w1_raw[:, a], w1_rows[a])
        base_t = held([PARTS, PACK], F32, "base_t")
        nc.gpsimd.dma_start(gain_t[:], gain.rearrange("(p t) -> p t", t=PACK))
        for q in range(4):
            nc.gpsimd.dma_start(
                w2_scales_raw[32 * q : 32 * q + 4, :, :].bitcast(I32),
                w2_scales[:, 4 * q : 4 * q + 4, :].rearrange("a r c -> r a c").bitcast(I32),
            )
        nc.gpsimd.dma_start(base_t[:], base.rearrange("(p t) -> p t", t=PACK))

        picked = [
            [over.tile([PARTS, BANK], U32, name=f"picked0{hf}", offset=2048 * hf, align_bytes=64) for hf in range(2)],
            [held([PARTS, BANK], U32, "picked10"), held([PARTS, BANK], U32, "picked11")],
        ]

        def pick_words(a):
            for hf in range(2):
                nc.vector.tensor_copy(
                    picked[a][hf][:], table[a][:].indirect(offs_t[:, hf * 32 : (hf + 1) * 32])
                )

        picked_scales = held([PARTS, S], U8, "picked_scales")
        nc.vector.tensor_copy(picked_scales[:], table_scales[:].indirect(offs_t[:]))
        for a in range(PASSES):
            for q in range(4):
                first = 64 * a + 16 * q
                nc.scalar.dma_start(
                    picked_plane[32 * q : 32 * q + 4, a, :].bitcast(I32),
                    picked_scales[first : first + 16 : 4, :].bitcast(I32),
                )
        pick_words(0)
        w2_plane = held([PARTS, PASSES, PACK, 128], U8, "w2_plane", "slot_d")
        nc.vector.tensor_copy(w2_plane[:], w2_scales_raw[:].rearrange("p a (m t) -> p a t m", t=PACK))
        pick_words(1)
        wash_t = held([PARTS, PACK, P], F32, "wash_t", "slot_a")
        nc.sync.dma_start(wash_t[:], wash.rearrange("(p t) j -> p t j", t=PACK))

        linear = [held([PARTS, S], F32, f"linear{t}") for t in range(PACK)]

        def bank(name, number, shape):
            return psum.tile(shape, F32, name=name, tag=f"bank{number}")

        def linear_part(unit):
            t, hf = divmod(unit, 2)
            cols = slice(hf * BANK, (hf + 1) * BANK)
            e2 = bank("e2", unit, [PARTS, BANK])
            for a in range(PASSES):
                nc.tensor.matmul_mx(
                    e2[:], w2_codes[:, a, 256 * t : 256 * (t + 1)].bitcast(E2M1), w2_plane[:, a, t, :],
                    picked[a][hf][:].bitcast(E4M3), picked_plane[:, a, cols],
                    start=(a == 0), stop=(a == PASSES - 1),
                )
            nc.scalar.activation(linear[t][:, cols], e2[:], ACT.Copy, scale=gain_t[:, t : t + 1])

        for unit in range(LINEAR_AHEAD):
            linear_part(unit)

        w1_bf = [held([PARTS, PACK, 128, PACK], BF16, f"w1_bf{a}", ("slot_b", "slot_f")[a]) for a in range(PASSES)]
        w1_codes = [held([PARTS, H], U32, f"w1_codes{a}") for a in range(PASSES)]
        w1_plane = [held([PARTS, H], U8, f"w1_plane{a}") for a in range(PASSES)]

        def weave_w1(copy, a, lo, hi):
            copy(
                w1_bf[a][:, lo:hi].rearrange("p t m j -> p m t j"),
                w1_raw[:, a].rearrange("p j (m t) -> p m t j", t=PACK)[:, :, lo:hi, :],
            )

        def quantise_w1(a, lo, hi):
            cols = slice(128 * lo, 128 * hi)
            nc.vector.quantize_mx(
                w1_codes[a][:, cols].bitcast(E4M3), w1_plane[a][:, cols],
                w1_bf[a][:, lo:hi].rearrange("p t m j -> p (t m j)"),
            )

        weave_w1(nc.vector.tensor_copy, 0, 0, PACK)
        quantise_w1(0, 0, PACK)
        weave_w1(nc.vector.tensor_copy, 1, 0, 2)
        weave_w1(nc.scalar.copy, 1, 2, PACK)
        quantise_w1(1, 0, 1)
        quantise_w1(1, 1, 2)
        quantise_w1(1, 2, PACK)

        w3_rows = w3.rearrange("(p t) n -> p t n", t=PACK)
        w3_raw = held([PARTS, PACK, N], F32, "w3_raw", "slot_e")
        nc.sync.dma_start(w3_raw[:], w3_rows)
        w4_codes = held([PARTS, 2 * N], U8, "w4_codes", "slot_b")
        nc.sync.dma_start(w4_codes[:].bitcast(I32), w4_words[0].bitcast(I32))
        w4_plane = held([PARTS, N], U8, "w4_plane", "slot_f")
        nc.gpsimd.memset(w4_plane[:].bitcast(I32), 0)
        for q in range(4):
            nc.sync.dma_start(
                w4_plane[32 * q : 32 * q + 4, :].bitcast(I32),
                w4_scales[0, 4 * q : 4 * q + 4, :].bitcast(I32),
            )

        h = [held([PARTS, S], F32, f"h{t}") for t in range(PACK)]
        xa_low = held([PARTS, 2, P], BF16, "xa_low")
        xb_f32 = [held([PARTS, 2, P], F32, f"xb_f32{u}") for u in range(2)]
        w3_codes = held([PARTS, N], U32, "w3_codes")
        w3_plane = held([PARTS, N], U8, "w3_plane")

        def features(t, hf):
            cols = slice(hf * BANK, (hf + 1) * BANK)
            rows = slice(t * 128, (t + 1) * 128)
            e1 = bank("e1", (2 * t + hf + 3) % 8, [PARTS, BANK])
            for a in range(PASSES):
                nc.tensor.matmul_mx(
                    e1[:], w1_codes[a][:, rows].bitcast(E4M3), w1_plane[a][:, rows],
                    picked[a][hf][:].bitcast(E4M3), picked_plane[:, a, cols],
                    start=(a == 0), stop=(a == PASSES - 1),
                )
            turns = work.tile([PARTS, BANK], F32, name="turns", bufs=2 * PACK)
            whole = work.tile([PARTS, BANK], I32, name="whole", bufs=2 * PACK)
            if hf == 0 and t > 0:
                rest = held([PARTS, BANK], F32, f"rest{t}", f"after_sin{t}")
                cosine = late.tile([PARTS, BANK], F32, name=f"cosine{t}", offset=COS_AT[t], align_bytes=64)
                wave = xb_f32[(t - 1) // 2][:, (t - 1) % 2, :]
            else:
                rest = work.tile([PARTS, BANK], F32, name="rest")
                cosine = work.tile([PARTS, BANK], F32, name="cosine")
                wave_tile = work.tile([PARTS, BANK], F32, name="wave_tile")
                wave = wave_tile[:]
            nc.scalar.activation(turns[:], e1[:], ACT.Copy, bias=0.25, scale=1.0 / (2.0 * math.pi))
            nc.gpsimd.tensor_scalar(whole[:], turns[:], 1.0, 0.0, ALU.mult, ALU.add)
            nc.vector.scalar_tensor_tensor(rest[:], whole[:], -2.0 * math.pi, e1[:], ALU.mult, ALU.add)
            nc.scalar.activation(cosine[:], rest[:], ACT.Sin, bias=math.pi / 2.0, scale=1.0)
            nc.vector.scalar_tensor_tensor(wave, cosine[:], gain_t[:, t : t + 1], e1[:], ALU.mult, ALU.mult)
            if 2 * t + hf + LINEAR_AHEAD < 2 * PACK:
                linear_part(2 * t + hf + LINEAR_AHEAD)
            adder = nc.vector if 2 * t + hf == 2 * PACK - 1 else nc.gpsimd
            adder.tensor_tensor(h[t][:, cols], wave, linear[t][:, cols], ALU.add)

        near = {}

        def pick(t, lo, hi):
            entries = slice(lo // 16, hi // 16)
            if t not in near:
                near[t] = late.tile([PARTS, P], F32, name=f"near{t}", offset=NEAR_AT[t], align_bytes=64)
            nc.vector.tensor_tensor(
                xb_f32[t // 2][:, t % 2, lo:hi], h[t][:].indirect(pos2_t[:, entries]), wash_t[:, t, lo:hi], ALU.add
            )
            nc.vector.tensor_copy(near[t][:, lo:hi], h[t][:].indirect(pos1_t[:, entries]))
            target = xa_low[:, t, lo:hi] if t < 2 else xa[:, lo:hi, t]
            nc.vector.tensor_scalar_max(target, near[t][:, lo:hi], base_t[:, t : t + 1])

        def weave_xb(u, lo, hi):
            nc.scalar.copy(xb[:, lo:hi, 2 * u : 2 * u + 2], xb_f32[u][:, :, lo:hi].rearrange("p t j -> p j t"))

        def prepare_w3(c):
            w3_bf = held([PARTS, N // 2, PACK], BF16, f"w3_bf{c}", f"after_sin{c + 1}")
            for lo in (0, N // 4):
                n0 = c * (N // 2) + lo
                nc.scalar.copy(
                    w3_bf[:, lo : lo + N // 4, :].rearrange("p (g i) t -> p g t i", i=4),
                    w3_raw[:, :, n0 : n0 + N // 4].rearrange("p t (g i) -> p g t i", i=4),
                )
            cols = slice(c * (N // 2), (c + 1) * (N // 2))
            nc.vector.quantize_mx(
                w3_codes[:, cols].bitcast(E4M3), w3_plane[:, cols], w3_bf[:].rearrange("p n t -> p (n t)")
            )

        for t in range(PACK):
            for hf in range(2):
                features(t, hf)
            if t == PACK - 1:
                xa = late.tile([PARTS, P, PACK], BF16, name="xa", offset=0, align_bytes=64)
                xb = held([PARTS, P, PACK], BF16, "xb", f"after_sin{t}")
            if t >= 1:
                pick(t - 1, 0, P)
            if t in (1, 2):
                prepare_w3(t - 1)
        weave_xb(0, 0, P)
        nc.scalar.copy(xa[:, :, 0:2], xa_low[:].rearrange("p t j -> p j t"))

        xa_codes = held([PARTS, P], U32, "xa_codes")
        xb_codes = held([PARTS, P], U32, "xb_codes")
        xa_plane = held([PARTS, P], U8, "xa_plane")
        xb_plane = held([PARTS, P], U8, "xb_plane")
        for hf in range(2):
            pick(PACK - 1, hf * HALF, (hf + 1) * HALF)
            weave_xb(1, hf * HALF, (hf + 1) * HALF)
            cols = slice(hf * HALF, (hf + 1) * HALF)
            for codes, plane, x in ((xa_codes, xa_plane, xa), (xb_codes, xb_plane, xb)):
                nc.vector.quantize_mx(
                    codes[:, cols].bitcast(E4M3), plane[:, cols], x[:, cols, :].rearrange("p j t -> p (j t)")
                )
        for hf in range(2):
            cols = slice(hf * HALF, (hf + 1) * HALF)
            for pair in range(N // 256):
                ya = bank("ya", (3 + 2 * (3 * hf + pair)) % 8, [PARTS, 2, HALF])
                yb = bank("yb", (4 + 2 * (3 * hf + pair)) % 8, [PARTS, 2, HALF])
                for i in range(2):
                    n0 = (2 * pair + i) * 128
                    nc.tensor.matmul_mx(
                        ya[:, i, :], w3_codes[:, n0 : n0 + 128].bitcast(E4M3), w3_plane[:, n0 : n0 + 128],
                        xa_codes[:, cols].bitcast(E4M3), xa_plane[:, cols], start=True, stop=True,
                    )
                for i in range(2):
                    n0 = (2 * pair + i) * 128
                    nc.tensor.matmul_mx(
                        yb[:, i, :], w4_codes[:, 2 * n0 : 2 * n0 + 256].bitcast(E2M1), w4_plane[:, n0 : n0 + 128],
                        xb_codes[:, cols].bitcast(E4M3), xb_plane[:, cols], start=True, stop=True,
                    )
                ya_s = work.tile([PARTS, 2, HALF], F32, name="ya_s")
                score = work.tile([PARTS, 2, HALF], F32, name="score")
                nc.scalar.copy(ya_s[:], ya[:])
                nc.vector.tensor_tensor(score[:], ya_s[:], yb[:], ALU.min)
                nc.sync.dma_start(
                    out[pair * 256 : (pair + 1) * 256, cols].rearrange("(i p) j -> p i j", i=2), score[:]
                )
